import numpy as np
import ml_dtypes


def mxq(x, axis, fmt="e4m3"):
    dtype, down = {"e4m3": (ml_dtypes.float8_e4m3fn, 7), "e5m2": (ml_dtypes.float8_e5m2, 14)}[fmt]
    v = np.moveaxis(np.asarray(x, np.float32).astype(ml_dtypes.bfloat16).astype(np.float64), axis, -1)
    blocks = v.reshape(v.shape[:-1] + (-1, 32))
    amax = np.abs(blocks).max(-1, keepdims=True)
    byte = np.maximum(np.where(amax > 0, np.frexp(amax)[1] - 1 + 127, 0) - down, 1)
    scale = np.exp2(byte - 127.0)
    codes = (blocks / scale).astype(np.float32).astype(dtype).astype(np.float64)
    return np.moveaxis((codes * scale).reshape(v.shape), -1, axis)


WIDE = False


def mx_kscale(k):
    if not WIDE:
        return np.ones(k)
    levels = np.array([10, -10, 5, -5, 0])
    if k % 512:
        return np.exp2(np.random.permutation(np.resize(levels, k // 32))).repeat(32)
    a = np.empty((k // 512, 16))
    for p in range(k // 512):
        a[p, :8] = np.random.permutation(np.resize(levels, 8))
        for g in range(8):
            far = levels[np.abs(levels - a[p, g]) >= 10]
            a[p, g + 8] = far[np.random.randint(len(far))]
    return np.exp2(a.ravel()).repeat(32)


def f64(x):
    return np.asarray(x).astype(np.float64)


def striped(idx):
    return np.tile(idx.reshape(-1, 16).T, (8, 1)).astype(np.uint16)


def unstriped(offs):
    return offs[:16].T.reshape(-1).astype(np.int64)


def pack_weight(w):
    k, n = w.shape
    w = f64(np.asarray(w, np.float32).astype(ml_dtypes.bfloat16)).reshape(k // 32, 32, n)
    amax = np.abs(w).max(1)
    byte = np.clip(np.where(amax > 0, np.frexp(amax)[1] - 1 + 127 - 7, 1), 1, 254)
    scaled = (w * np.exp2(127.0 - byte)[:, None, :]).reshape(k, n).astype(np.float32)
    words = np.ascontiguousarray(scaled.reshape(k // 512, 128, 4, n).transpose(0, 1, 3, 2)).astype(ml_dtypes.float8_e4m3fn).view(np.uint8)
    return words, np.ascontiguousarray(byte.astype(np.uint8).reshape(k // 512, 16, n))


def unpack_weight(words, scales):
    g, p, n, _ = words.shape
    vals = np.ascontiguousarray(words).view(ml_dtypes.float8_e4m3fn).astype(np.float64) * np.repeat(np.exp2(scales.astype(np.float64) - 127.0), 8, axis=1)[..., None]
    return vals.transpose(0, 1, 3, 2).reshape(g * 512, n)


def relu(v):
    return np.maximum(v, 0.0)


def sigmoid(v):
    return 1.0 / (1.0 + np.exp(-np.maximum(v, -700.0)))


K, T, S, N = 512, 2048, 1024, 256


def setup_inputs():
    n = np.random.standard_normal
    s = mx_kscale(K)[:, None]
    packed_w1 = pack_weight(n((K, N)) / np.sqrt(K) / s)
    packed_w2 = pack_weight(n((K, N)) / np.sqrt(K) / s)
    return {
        "xT": (n((K, T)) * s).astype(np.float32),
        "res": n((N, T)).astype(np.float32),
        "w1_words": packed_w1[0],
        "w1_scales": packed_w1[1],
        "w2_words": packed_w2[0],
        "w2_scales": packed_w2[1],
        "offs": striped(np.random.permutation(T)[:S]),
    }


def reference(xT, res, w1_words, w1_scales, w2_words, w2_scales, offs):
    r = f64(res)[:, unstriped(offs)]
    xq = mxq(f64(xT)[:, unstriped(offs)], 0, "e4m3")
    g = sigmoid(unpack_weight(w2_words, w2_scales).T @ xq)
    y = relu(unpack_weight(w1_words, w1_scales).T @ xq)
    return r + g * (y - r)

@@ -1,0 +1,170 @@
+from contextlib import ExitStack
+
+import concourse.mybir as mybir
+
+K, T, S, N = 512, 2048, 1024, 256
+FLOPS = 2 * 2 * K * N * S
+
+F32 = mybir.dt.float32
+BF16 = mybir.dt.bfloat16
+U32 = mybir.dt.uint32
+I32 = mybir.dt.int32
+U16 = mybir.dt.uint16
+U8 = mybir.dt.uint8
+FP8X4 = mybir.dt.float8_e4m3fn_x4
+ALU = mybir.AluOpType
+ACT = mybir.ActivationFunctionType
+
+P = 128
+SL = 256
+NS = S // SL
+CHUNKS = [[1024, 1024], [512, 512, 512, 512]]
+
+
+def tile_picked_highway_relu_l_kernel(tc, xT, res, w1_words, w1_scales, w2_words, w2_scales, offs, out):
+    nc = tc.nc
+    with ExitStack() as ctx:
+        keep = ctx.enter_context(tc.tile_pool(name="keep", bufs=1))
+        psum = ctx.enter_context(tc.psum_pool(name="psum", bufs=1))
+
+        offsets = keep.tile([P, S // 16], U16, name="offsets")
+        w_scale = keep.tile([P, 2 * N], U8, name="w_scale", align_bytes=64)
+        w_code = [keep.tile([P, N], U32, name=f"w_code{i}", align_bytes=64) for i in range(2)]
+        warm_in = keep.tile([P, 8], F32, name="warm_in")
+        warm_out = keep.tile([P, 8], F32, name="warm_out")
+
+        w_scale_i = w_scale[:].bitcast(I32)
+        nc.vector.memset(w_scale_i, 0)
+        nc.vector.memset(warm_in[:], 0.0)
+        nc.scalar.activation(warm_out[:], warm_in[:], ACT.Sigmoid)
+
+        def load_scales(queue, i, scales):
+            for q in range(4):
+                queue.dma_start(
+                    out=w_scale_i[32 * q : 32 * q + 4, i * (N // 4) : (i + 1) * (N // 4)],
+                    in_=scales[0, 4 * q : 4 * q + 4, :].bitcast(I32),
+                )
+
+        x_rows = xT.rearrange("(p j) t -> p j t", j=4)
+        raw = []
+        for u in range(2):
+            c0 = 0
+            for c, width in enumerate(CHUNKS[u]):
+                piece = keep.tile([P, 2, width], F32, name=f"raw{u}_{c}")
+                nc.sync.dma_start(out=piece[:], in_=x_rows[:, 2 * u : 2 * u + 2, c0 : c0 + width])
+                raw.append((u, c, c0, width, piece))
+                if u == 0 and c == 0:
+                    load_scales(nc.sync, 1, w2_scales)
+                    nc.sync.dma_start(offsets[:], offs)
+                c0 += width
+        for i, words in ((1, w2_words), (0, w1_words)):
+            nc.sync.dma_start(out=w_code[i][:].bitcast(I32), in_=words[0].rearrange("p n t -> p (n t)").bitcast(I32))
+        res_sb = [keep.tile([P, T], F32, name=f"res{m}") for m in range(2)]
+        for m in range(2):
+            nc.sync.dma_start(out=res_sb[m][:], in_=res[m * P : (m + 1) * P, :])
+
+        load_scales(nc.gpsimd, 0, w1_scales)
+
+        pair = [keep.tile([P, 2 * T], BF16, name=f"pair{u}", align_bytes=64) for u in range(2)]
+
+        def cast(engine, u, c0, piece, a, b):
+            dst = pair[u][:, 2 * (c0 + a) : 2 * (c0 + b)].rearrange("p (t e) -> p t e", e=2)
+            src = piece[:, :, a:b].rearrange("p e t -> p t e")
+            if engine == "v":
+                nc.vector.tensor_copy(out=dst, in_=src)
+            else:
+                nc.scalar.copy(out=dst, in_=src)
+
+        picked = [keep.tile([P, 2, SL], U32, name=f"picked{s}") for s in range(NS)]
+
+        def lists(a, b):
+            return offsets[:, a // 16 : b // 16]
+
+        for u, c, c0, width, piece in raw:
+            if u == 0:
+                cast("v", u, c0, piece, 0, width)
+                if c == 1:
+                    for s in range(NS):
+                        nc.vector.tensor_copy(out=picked[s][:, 0, :], in_=pair[0][:].bitcast(U32).indirect(lists(s * SL, (s + 1) * SL)))
+            elif c < 2:
+                cast("s", u, c0, piece, 0, width)
+            elif c == 2:
+                cast("v", u, c0, piece, 0, width)
+            else:
+                cast("v", u, c0, piece, 0, 320)
+                cast("s", u, c0, piece, 320, width)
+
+        woven = [keep.tile([P, 4 * SL], BF16, name=f"woven{s}", align_bytes=64) for s in range(NS)]
+        codes = [keep.tile([P, SL], U32, name=f"codes{s}", align_bytes=64) for s in range(NS)]
+        x_scale = [keep.tile([P, SL], U8, name=f"x_scale{s}", align_bytes=64) for s in range(NS)]
+        bank = [[psum.tile([P, 2, SL], F32, name=f"bank{i}_{s}") for s in range(NS)] for i in range(2)]
+        gate = [keep.tile([P, 2, SL], F32, name=f"gate{s}") for s in range(NS)]
+        carry = [keep.tile([P, 2, SL], F32, name=f"carry{s}") for s in range(NS)]
+        made = [keep.tile([P, 2, SL], F32, name=f"made{h}") for h in range(NS)]
+        passed = [[keep.tile([P, SL], F32, name=f"passed{m}_{s}") for s in range(NS)] for m in range(2)]
+        result = [[keep.tile([P, SL], F32, name=f"result{m}_{s}") for s in range(NS)] for m in range(2)]
+
+        def gather(s):
+            nc.vector.tensor_copy(out=picked[s][:, 1, :], in_=pair[1][:].bitcast(U32).indirect(lists(s * SL, (s + 1) * SL)))
+            nc.scalar.copy(
+                out=woven[s][:].bitcast(U32).rearrange("p (t u) -> p t u", u=2),
+                in_=picked[s][:].rearrange("p u t -> p t u"),
+            )
+
+        def multiply(s):
+            nc.vector.quantize_mx(out=codes[s][:].bitcast(FP8X4), scales=x_scale[s][:], in_=woven[s][:])
+            for i in (1, 0):
+                for m in range(2):
+                    nc.tensor.matmul_mx(
+                        out=bank[i][s][:, m, :],
+                        lhsT=w_code[i][:, m * P : (m + 1) * P].bitcast(FP8X4),
+                        lhsT_scale=w_scale[:, i * N + m * P : i * N + (m + 1) * P],
+                        rhs=codes[s][:].bitcast(FP8X4),
+                        rhs_scale=x_scale[s][:],
+                        start=True,
+                        stop=True,
+                    )
+
+        def gates(s):
+            nc.scalar.activation(carry[s][:], bank[1][s][:], ACT.Sigmoid, scale=-1.0)
+            nc.scalar.activation(gate[s][:], bank[1][s][:], ACT.Sigmoid)
+
+        def layer(s):
+            nc.vector.scalar_tensor_tensor(out=made[s][:], in0=bank[0][s][:], scalar=0.0, in1=gate[s][:], op0=ALU.max, op1=ALU.mult)
+
+        def highway(m, s):
+            nc.vector.tensor_tensor(passed[m][s][:], res_sb[m][:].indirect(lists(s * SL, (s + 1) * SL)), carry[s][:, m, :], ALU.mult)
+
+        def finish(m, s):
+            nc.vector.tensor_tensor(result[m][s][:], passed[m][s][:], made[s][:, m, :], ALU.add)
+            nc.sync.dma_start(out=out[m * P : (m + 1) * P, s * SL : (s + 1) * SL], in_=result[m][s][:])
+
+        gather(0)
+        gather(1)
+        multiply(0)
+        gather(2)
+        multiply(1)
+        gather(3)
+        gates(0)
+        multiply(2)
+        highway(0, 0)
+        gates(1)
+        multiply(3)
+        layer(0)
+        gates(2)
+        highway(0, 1)
+        finish(0, 0)
+        layer(1)
+        gates(3)
+        highway(0, 2)
+        finish(0, 1)
+        layer(2)
+        highway(0, 3)
+        finish(0, 2)
+        layer(3)
+        highway(1, 0)
+        finish(0, 3)
+        for s in range(1, NS):
+            highway(1, s)
+            finish(1, s - 1)
+        finish(1, NS - 1)

@@ -1,6 +1,7 @@
 from contextlib import ExitStack
 
 import concourse.mybir as mybir
+from concourse.masks import make_identity
 
 K, T, S, N = 512, 2048, 1024, 256
 FLOPS = 2 * 2 * K * N * S
@@ -18,7 +19,7 @@ ACT = mybir.ActivationFunctionType
 P = 128
 SL = 256
 NS = S // SL
-CHUNKS = [[1024, 1024], [512, 512, 512, 512]]
+CHUNKS = [[1024, 1024], [512, 512, 640, 384]]
 
 
 def tile_picked_highway_relu_l_kernel(tc, xT, res, w1_words, w1_scales, w2_words, w2_scales, offs, out):
@@ -34,6 +35,7 @@ def tile_picked_highway_relu_l_kernel(tc, xT, res, w1_words, w1_scales, w2_words
         warm_out = keep.tile([P, 8], F32, name="warm_out")
 
         w_scale_i = w_scale[:].bitcast(I32)
+        staged = keep.tile([P, 2 * N // 4], I32, name="staged")
         nc.vector.memset(w_scale_i, 0)
         nc.vector.memset(warm_in[:], 0.0)
         nc.scalar.activation(warm_out[:], warm_in[:], ACT.Sigmoid)
@@ -41,7 +43,7 @@ def tile_picked_highway_relu_l_kernel(tc, xT, res, w1_words, w1_scales, w2_words
         def load_scales(queue, i, scales):
             for q in range(4):
                 queue.dma_start(
-                    out=w_scale_i[32 * q : 32 * q + 4, i * (N // 4) : (i + 1) * (N // 4)],
+                    out=staged[32 * q : 32 * q + 4, i * (N // 4) : (i + 1) * (N // 4)],
                     in_=scales[0, 4 * q : 4 * q + 4, :].bitcast(I32),
                 )
 
@@ -54,7 +56,7 @@ def tile_picked_highway_relu_l_kernel(tc, xT, res, w1_words, w1_scales, w2_words
                 nc.sync.dma_start(out=piece[:], in_=x_rows[:, 2 * u : 2 * u + 2, c0 : c0 + width])
                 raw.append((u, c, c0, width, piece))
                 if u == 0 and c == 0:
-                    load_scales(nc.sync, 1, w2_scales)
+                    load_scales(nc.scalar, 1, w2_scales)
                     nc.sync.dma_start(offsets[:], offs)
                 c0 += width
         for i, words in ((1, w2_words), (0, w1_words)):
@@ -64,6 +66,11 @@ def tile_picked_highway_relu_l_kernel(tc, xT, res, w1_words, w1_scales, w2_words
             nc.sync.dma_start(out=res_sb[m][:], in_=res[m * P : (m + 1) * P, :])
 
         load_scales(nc.gpsimd, 0, w1_scales)
+        for q in range(4):
+            nc.gpsimd.tensor_copy(out=w_scale_i[32 * q : 32 * q + 4, :], in_=staged[32 * q : 32 * q + 4, :])
+
+        ident = keep.tile([P, P], F32, name="ident")
+        make_identity(nc, ident[:])
 
         pair = [keep.tile([P, 2 * T], BF16, name=f"pair{u}", align_bytes=64) for u in range(2)]
 
@@ -75,96 +82,132 @@ def tile_picked_highway_relu_l_kernel(tc, xT, res, w1_words, w1_scales, w2_words
             else:
                 nc.scalar.copy(out=dst, in_=src)
 
-        picked = [keep.tile([P, 2, SL], U32, name=f"picked{s}") for s in range(NS)]
+        lane = [keep.tile([P, 3, SL], U32, name=f"lane{s}") for s in range(2)]
 
         def lists(a, b):
             return offsets[:, a // 16 : b // 16]
 
         for u, c, c0, width, piece in raw:
-            if u == 0:
-                cast("v", u, c0, piece, 0, width)
-                if c == 1:
-                    for s in range(NS):
-                        nc.vector.tensor_copy(out=picked[s][:, 0, :], in_=pair[0][:].bitcast(U32).indirect(lists(s * SL, (s + 1) * SL)))
-            elif c < 2:
+            if u == 1 and c < 2:
                 cast("s", u, c0, piece, 0, width)
-            elif c == 2:
-                cast("v", u, c0, piece, 0, width)
             else:
-                cast("v", u, c0, piece, 0, 320)
-                cast("s", u, c0, piece, 320, width)
+                cast("v", u, c0, piece, 0, width * 5 // 8)
+                cast("s", u, c0, piece, width * 5 // 8, width)
+            if u == 0 and c == 1:
+                for s in range(NS):
+                    nc.vector.tensor_copy(out=lane[s % 2][:, 1 - s // 2, :], in_=pair[0][:].bitcast(U32).indirect(lists(s * SL, (s + 1) * SL)))
 
         woven = [keep.tile([P, 4 * SL], BF16, name=f"woven{s}", align_bytes=64) for s in range(NS)]
-        codes = [keep.tile([P, SL], U32, name=f"codes{s}", align_bytes=64) for s in range(NS)]
-        x_scale = [keep.tile([P, SL], U8, name=f"x_scale{s}", align_bytes=64) for s in range(NS)]
-        bank = [[psum.tile([P, 2, SL], F32, name=f"bank{i}_{s}") for s in range(NS)] for i in range(2)]
-        gate = [keep.tile([P, 2, SL], F32, name=f"gate{s}") for s in range(NS)]
-        carry = [keep.tile([P, 2, SL], F32, name=f"carry{s}") for s in range(NS)]
-        made = [keep.tile([P, 2, SL], F32, name=f"made{h}") for h in range(NS)]
-        passed = [[keep.tile([P, SL], F32, name=f"passed{m}_{s}") for s in range(NS)] for m in range(2)]
-        result = [[keep.tile([P, SL], F32, name=f"result{m}_{s}") for s in range(NS)] for m in range(2)]
+        codes = keep.tile([P, S], U32, name="codes", align_bytes=64)
+        x_scale = keep.tile([P, S], U8, name="x_scale", align_bytes=64)
+        bank = [psum.tile([P, 2, SL], F32, name=f"bank{s}", tag=f"bank0_{s}") for s in range(NS)]
+        wide = [[psum.tile([P, 2 * SL], F32, name=f"wide{i}_{h}") for h in range(2)] for i in range(2)]
+        gate = [keep.tile([P, S], F32, name=f"gate{m}") for m in range(2)]
+        carry = [keep.tile([P, S], F32, name=f"carry{m}") for m in range(2)]
+        made = [keep.tile([P, S], F32, name=f"made{m}") for m in range(2)]
+        passed = [keep.tile([P, S], F32, name=f"passed{m}") for m in range(2)]
+        result = [keep.tile([P, S], F32, name=f"result{m}") for m in range(2)]
+        turned = keep.tile([P, S], F32, name="turned")
 
         def gather(s):
-            nc.vector.tensor_copy(out=picked[s][:, 1, :], in_=pair[1][:].bitcast(U32).indirect(lists(s * SL, (s + 1) * SL)))
+            nc.vector.tensor_copy(out=lane[s % 2][:, 2, :], in_=pair[1][:].bitcast(U32).indirect(lists(s * SL, (s + 1) * SL)))
             nc.scalar.copy(
                 out=woven[s][:].bitcast(U32).rearrange("p (t u) -> p t u", u=2),
-                in_=picked[s][:].rearrange("p u t -> p t u"),
+                in_=lane[s % 2][:, 1 - s // 2 : 3 : 1 + s // 2, :].rearrange("p u t -> p t u"),
             )
 
-        def multiply(s):
-            nc.vector.quantize_mx(out=codes[s][:].bitcast(FP8X4), scales=x_scale[s][:], in_=woven[s][:])
+        def quantise(s):
+            cols = slice(s * SL, (s + 1) * SL)
+            nc.vector.quantize_mx(out=codes[:, cols].bitcast(FP8X4), scales=x_scale[:, cols], in_=woven[s][:])
+
+        def sums(i, m, a, b):
+            if m == 0:
+                return bank[a // SL][:, i, :]
+            return wide[i][a // (2 * SL)][:]
+
+        def multiply(m, a, b):
             for i in (1, 0):
-                for m in range(2):
-                    nc.tensor.matmul_mx(
-                        out=bank[i][s][:, m, :],
-                        lhsT=w_code[i][:, m * P : (m + 1) * P].bitcast(FP8X4),
-                        lhsT_scale=w_scale[:, i * N + m * P : i * N + (m + 1) * P],
-                        rhs=codes[s][:].bitcast(FP8X4),
-                        rhs_scale=x_scale[s][:],
-                        start=True,
-                        stop=True,
-                    )
+                nc.tensor.matmul_mx(
+                    out=sums(i, m, a, b),
+                    lhsT=w_code[i][:, m * P : (m + 1) * P].bitcast(FP8X4),
+                    lhsT_scale=w_scale[:, i * N + m * P : i * N + (m + 1) * P],
+                    rhs=codes[:, a:b].bitcast(FP8X4),
+                    rhs_scale=x_scale[:, a:b],
+                    start=True,
+                    stop=True,
+                )
 
-        def gates(s):
-            nc.scalar.activation(carry[s][:], bank[1][s][:], ACT.Sigmoid, scale=-1.0)
-            nc.scalar.activation(gate[s][:], bank[1][s][:], ACT.Sigmoid)
+        def gates(m, a, b):
+            nc.scalar.activation(carry[m][:, a:b], sums(1, m, a, b), ACT.Sigmoid, scale=-1.0)
+            nc.scalar.activation(gate[m][:, a:b], sums(1, m, a, b), ACT.Sigmoid)
 
-        def layer(s):
-            nc.vector.scalar_tensor_tensor(out=made[s][:], in0=bank[0][s][:], scalar=0.0, in1=gate[s][:], op0=ALU.max, op1=ALU.mult)
+        def highway(m, a, b):
+            nc.vector.tensor_tensor(passed[m][:, a:b], res_sb[m][:].indirect(lists(a, b)), carry[m][:, a:b], ALU.mult)
 
-        def highway(m, s):
-            nc.vector.tensor_tensor(passed[m][s][:], res_sb[m][:].indirect(lists(s * SL, (s + 1) * SL)), carry[s][:, m, :], ALU.mult)
+        def layer(m, a, b):
+            nc.vector.scalar_tensor_tensor(out=made[m][:, a:b], in0=sums(0, m, a, b), scalar=0.0, in1=gate[m][:, a:b], op0=ALU.max, op1=ALU.mult)
 
-        def finish(m, s):
-            nc.vector.tensor_tensor(result[m][s][:], passed[m][s][:], made[s][:, m, :], ALU.add)
-            nc.sync.dma_start(out=out[m * P : (m + 1) * P, s * SL : (s + 1) * SL], in_=result[m][s][:])
+        def store(m, a, b):
+            queue = nc.scalar if m == 0 else nc.sync
+            queue.dma_start(out=out[m * P : (m + 1) * P, a:b], in_=result[m][:, a:b])
+
+        def add_on_vector(m, a, b):
+            nc.vector.tensor_tensor(result[m][:, a:b], passed[m][:, a:b], made[m][:, a:b], ALU.add)
+            store(m, a, b)
+
+        def sum_turned(m, h):
+            summed = psum.tile([P, 2 * SL], F32, name=f"summed{h}", tag=f"bank{m}_{2 * h}")
+            for j in range(4):
+                cols = slice(2 * SL * h + P * j, 2 * SL * h + P * (j + 1))
+                for first, term in ((True, passed[m]), (False, made[m])):
+                    nc.tensor.matmul(summed[:, P * j : P * (j + 1)], lhsT=term[:, cols], rhs=ident[:], start=first, stop=not first, is_transpose=True)
+            nc.scalar.copy(out=turned[:, 2 * SL * h : 2 * SL * (h + 1)], in_=summed[:])
+
+        def turn_back(m, h):
+            back = psum.tile([P, 2 * SL], F32, name=f"back{h}", tag=f"bank{m}_{2 * h + 1}")
+            for j in range(4):
+                cols = slice(2 * SL * h + P * j, 2 * SL * h + P * (j + 1))
+                nc.tensor.transpose(back[:, P * j : P * (j + 1)], turned[:, cols], ident[:])
+            nc.scalar.copy(out=result[m][:, 2 * SL * h : 2 * SL * (h + 1)], in_=back[:])
+            store(m, 2 * SL * h, 2 * SL * (h + 1))
+
+        def terms(s):
+            highway(0, s * SL, (s + 1) * SL)
+            layer(0, s * SL, (s + 1) * SL)
 
         gather(0)
         gather(1)
-        multiply(0)
+        quantise(0)
+        multiply(0, 0, 256)
         gather(2)
-        multiply(1)
+        quantise(1)
+        multiply(0, 256, 512)
         gather(3)
-        gates(0)
-        multiply(2)
-        highway(0, 0)
-        gates(1)
-        multiply(3)
-        layer(0)
-        gates(2)
-        highway(0, 1)
-        finish(0, 0)
-        layer(1)
-        gates(3)
-        highway(0, 2)
-        finish(0, 1)
-        layer(2)
-        highway(0, 3)
-        finish(0, 2)
-        layer(3)
-        highway(1, 0)
-        finish(0, 3)
-        for s in range(1, NS):
-            highway(1, s)
-            finish(1, s - 1)
-        finish(1, NS - 1)
+        gates(0, 0, 256)
+        quantise(2)
+        multiply(0, 512, 768)
+        terms(0)
+        gates(0, 256, 512)
+        quantise(3)
+        multiply(0, 768, 1024)
+        multiply(1, 0, 512)
+        multiply(1, 512, 1024)
+        terms(1)
+        gates(0, 512, 768)
+        terms(2)
+        gates(0, 768, 1024)
+        terms(3)
+        gates(1, 0, 512)
+        sum_turned(0, 0)
+        highway(1, 0, 512)
+        layer(1, 0, 512)
+        gates(1, 512, 1024)
+        turn_back(0, 0)
+        sum_turned(0, 1)
+        layer(1, 512, 1024)
+        highway(1, 512, 768)
+        add_on_vector(1, 0, 512)
+        turn_back(0, 1)
+        highway(1, 768, 1024)
+        add_on_vector(1, 512, 768)
+        add_on_vector(1, 768, 1024)

@@ -19,7 +19,7 @@ ACT = mybir.ActivationFunctionType
 P = 128
 SL = 256
 NS = S // SL
-CHUNKS = [[1024, 1024], [512, 512, 640, 384]]
+CHUNKS = [[1024, 1024], [1024, 640, 384]]
 
 
 def tile_picked_highway_relu_l_kernel(tc, xT, res, w1_words, w1_scales, w2_words, w2_scales, offs, out):
@@ -82,26 +82,28 @@ def tile_picked_highway_relu_l_kernel(tc, xT, res, w1_words, w1_scales, w2_words
             else:
                 nc.scalar.copy(out=dst, in_=src)
 
-        lane = [keep.tile([P, 3, SL], U32, name=f"lane{s}") for s in range(2)]
+        lane = [keep.tile([P, 3, SL], U32, name=f"lane{s}") for s in range(3)]
 
         def lists(a, b):
             return offsets[:, a // 16 : b // 16]
 
         for u, c, c0, width, piece in raw:
-            if u == 1 and c < 2:
+            if u == 1 and c == 0:
                 cast("s", u, c0, piece, 0, width)
+            elif u == 1 and c == 1:
+                cast("v", u, c0, piece, 0, width)
             else:
                 cast("v", u, c0, piece, 0, width * 5 // 8)
                 cast("s", u, c0, piece, width * 5 // 8, width)
             if u == 0 and c == 1:
                 for s in range(NS):
-                    nc.vector.tensor_copy(out=lane[s % 2][:, 1 - s // 2, :], in_=pair[0][:].bitcast(U32).indirect(lists(s * SL, (s + 1) * SL)))
+                    nc.vector.tensor_copy(out=lane[s % 3][:, 1 - s // 3, :], in_=pair[0][:].bitcast(U32).indirect(lists(s * SL, (s + 1) * SL)))
 
         woven = [keep.tile([P, 4 * SL], BF16, name=f"woven{s}", align_bytes=64) for s in range(NS)]
         codes = keep.tile([P, S], U32, name="codes", align_bytes=64)
         x_scale = keep.tile([P, S], U8, name="x_scale", align_bytes=64)
         bank = [psum.tile([P, 2, SL], F32, name=f"bank{s}", tag=f"bank0_{s}") for s in range(NS)]
-        wide = [[psum.tile([P, 2 * SL], F32, name=f"wide{i}_{h}") for h in range(2)] for i in range(2)]
+        wide = [[psum.tile([P, 2 * SL], F32, name=f"wide{i}_{h}", tag=f"bank1_{2 * h + i}") for h in range(2)] for i in range(2)]
         gate = [keep.tile([P, S], F32, name=f"gate{m}") for m in range(2)]
         carry = [keep.tile([P, S], F32, name=f"carry{m}") for m in range(2)]
         made = [keep.tile([P, S], F32, name=f"made{m}") for m in range(2)]
@@ -110,10 +112,10 @@ def tile_picked_highway_relu_l_kernel(tc, xT, res, w1_words, w1_scales, w2_words
         turned = keep.tile([P, S], F32, name="turned")
 
         def gather(s):
-            nc.vector.tensor_copy(out=lane[s % 2][:, 2, :], in_=pair[1][:].bitcast(U32).indirect(lists(s * SL, (s + 1) * SL)))
+            nc.vector.tensor_copy(out=lane[s % 3][:, 2, :], in_=pair[1][:].bitcast(U32).indirect(lists(s * SL, (s + 1) * SL)))
             nc.scalar.copy(
                 out=woven[s][:].bitcast(U32).rearrange("p (t u) -> p t u", u=2),
-                in_=lane[s % 2][:, 1 - s // 2 : 3 : 1 + s // 2, :].rearrange("p u t -> p t u"),
+                in_=lane[s % 3][:, 1 - s // 3 : 3 : 1 + s // 3, :].rearrange("p u t -> p t u"),
             )
 
         def quantise(s):
@@ -147,16 +149,15 @@ def tile_picked_highway_relu_l_kernel(tc, xT, res, w1_words, w1_scales, w2_words
         def layer(m, a, b):
             nc.vector.scalar_tensor_tensor(out=made[m][:, a:b], in0=sums(0, m, a, b), scalar=0.0, in1=gate[m][:, a:b], op0=ALU.max, op1=ALU.mult)
 
-        def store(m, a, b):
-            queue = nc.scalar if m == 0 else nc.sync
+        def store(queue, m, a, b):
             queue.dma_start(out=out[m * P : (m + 1) * P, a:b], in_=result[m][:, a:b])
 
         def add_on_vector(m, a, b):
             nc.vector.tensor_tensor(result[m][:, a:b], passed[m][:, a:b], made[m][:, a:b], ALU.add)
-            store(m, a, b)
+            store(nc.sync, m, a, b)
 
         def sum_turned(m, h):
-            summed = psum.tile([P, 2 * SL], F32, name=f"summed{h}", tag=f"bank{m}_{2 * h}")
+            summed = psum.tile([P, 2 * SL], F32, name=f"summed{m}_{h}", tag=f"bank{m}_{2 * h}")
             for j in range(4):
                 cols = slice(2 * SL * h + P * j, 2 * SL * h + P * (j + 1))
                 for first, term in ((True, passed[m]), (False, made[m])):
@@ -164,12 +165,12 @@ def tile_picked_highway_relu_l_kernel(tc, xT, res, w1_words, w1_scales, w2_words
             nc.scalar.copy(out=turned[:, 2 * SL * h : 2 * SL * (h + 1)], in_=summed[:])
 
         def turn_back(m, h):
-            back = psum.tile([P, 2 * SL], F32, name=f"back{h}", tag=f"bank{m}_{2 * h + 1}")
+            back = psum.tile([P, 2 * SL], F32, name=f"back{m}_{h}", tag=f"bank{m}_{2 * h + 1}")
             for j in range(4):
                 cols = slice(2 * SL * h + P * j, 2 * SL * h + P * (j + 1))
                 nc.tensor.transpose(back[:, P * j : P * (j + 1)], turned[:, cols], ident[:])
             nc.scalar.copy(out=result[m][:, 2 * SL * h : 2 * SL * (h + 1)], in_=back[:])
-            store(m, 2 * SL * h, 2 * SL * (h + 1))
+            store(nc.scalar, m, 2 * SL * h, 2 * SL * (h + 1))
 
         def terms(s):
             highway(0, s * SL, (s + 1) * SL)
@@ -177,12 +178,12 @@ def tile_picked_highway_relu_l_kernel(tc, xT, res, w1_words, w1_scales, w2_words
 
         gather(0)
         gather(1)
+        gather(2)
         quantise(0)
         multiply(0, 0, 256)
-        gather(2)
+        gather(3)
         quantise(1)
         multiply(0, 256, 512)
-        gather(3)
         gates(0, 0, 256)
         quantise(2)
         multiply(0, 512, 768)
@@ -205,9 +206,9 @@ def tile_picked_highway_relu_l_kernel(tc, xT, res, w1_words, w1_scales, w2_words
         turn_back(0, 0)
         sum_turned(0, 1)
         layer(1, 512, 1024)
-        highway(1, 512, 768)
+        highway(1, 512, 896)
         add_on_vector(1, 0, 512)
         turn_back(0, 1)
-        highway(1, 768, 1024)
-        add_on_vector(1, 512, 768)
-        add_on_vector(1, 768, 1024)
+        highway(1, 896, 1024)
+        add_on_vector(1, 512, 896)
+        add_on_vector(1, 896, 1024)

from contextlib import ExitStack

import concourse.mybir as mybir
from concourse.masks import make_identity

K, T, S, N = 512, 2048, 1024, 256
FLOPS = 2 * 2 * K * N * S

F32 = mybir.dt.float32
BF16 = mybir.dt.bfloat16
U32 = mybir.dt.uint32
I32 = mybir.dt.int32
U16 = mybir.dt.uint16
U8 = mybir.dt.uint8
FP8X4 = mybir.dt.float8_e4m3fn_x4
ALU = mybir.AluOpType
ACT = mybir.ActivationFunctionType

P = 128
SL = 256
NS = S // SL
CHUNKS = [[1024, 1024], [1024, 640, 384]]


def tile_picked_highway_relu_l_kernel(tc, xT, res, w1_words, w1_scales, w2_words, w2_scales, offs, out):
    nc = tc.nc
    with ExitStack() as ctx:
        keep = ctx.enter_context(tc.tile_pool(name="keep", bufs=1))
        psum = ctx.enter_context(tc.psum_pool(name="psum", bufs=1))

        offsets = keep.tile([P, S // 16], U16, name="offsets")
        w_scale = keep.tile([P, 2 * N], U8, name="w_scale", align_bytes=64)
        w_code = [keep.tile([P, N], U32, name=f"w_code{i}", align_bytes=64) for i in range(2)]
        warm_in = keep.tile([P, 8], F32, name="warm_in")
        warm_out = keep.tile([P, 8], F32, name="warm_out")

        w_scale_i = w_scale[:].bitcast(I32)
        staged = keep.tile([P, 2 * N // 4], I32, name="staged")
        nc.vector.memset(w_scale_i, 0)
        nc.vector.memset(warm_in[:], 0.0)
        nc.scalar.activation(warm_out[:], warm_in[:], ACT.Sigmoid)

        def load_scales(queue, i, scales):
            for q in range(4):
                queue.dma_start(
                    out=staged[32 * q : 32 * q + 4, i * (N // 4) : (i + 1) * (N // 4)],
                    in_=scales[0, 4 * q : 4 * q + 4, :].bitcast(I32),
                )

        x_rows = xT.rearrange("(p j) t -> p j t", j=4)
        raw = []
        for u in range(2):
            c0 = 0
            for c, width in enumerate(CHUNKS[u]):
                piece = keep.tile([P, 2, width], F32, name=f"raw{u}_{c}")
                nc.sync.dma_start(out=piece[:], in_=x_rows[:, 2 * u : 2 * u + 2, c0 : c0 + width])
                raw.append((u, c, c0, width, piece))
                if u == 0 and c == 0:
                    load_scales(nc.scalar, 1, w2_scales)
                    nc.sync.dma_start(offsets[:], offs)
                c0 += width
        for i, words in ((1, w2_words), (0, w1_words)):
            nc.sync.dma_start(out=w_code[i][:].bitcast(I32), in_=words[0].rearrange("p n t -> p (n t)").bitcast(I32))
        res_sb = [keep.tile([P, T], F32, name=f"res{m}") for m in range(2)]
        for m in range(2):
            nc.sync.dma_start(out=res_sb[m][:], in_=res[m * P : (m + 1) * P, :])

        load_scales(nc.gpsimd, 0, w1_scales)
        for q in range(4):
            nc.gpsimd.tensor_copy(out=w_scale_i[32 * q : 32 * q + 4, :], in_=staged[32 * q : 32 * q + 4, :])

        ident = keep.tile([P, P], F32, name="ident")
        make_identity(nc, ident[:])

        pair = [keep.tile([P, 2 * T], BF16, name=f"pair{u}", align_bytes=64) for u in range(2)]

        def cast(engine, u, c0, piece, a, b):
            dst = pair[u][:, 2 * (c0 + a) : 2 * (c0 + b)].rearrange("p (t e) -> p t e", e=2)
            src = piece[:, :, a:b].rearrange("p e t -> p t e")
            if engine == "v":
                nc.vector.tensor_copy(out=dst, in_=src)
            else:
                nc.scalar.copy(out=dst, in_=src)

        lane = [keep.tile([P, 3, SL], U32, name=f"lane{s}") for s in range(3)]

        def lists(a, b):
            return offsets[:, a // 16 : b // 16]

        for u, c, c0, width, piece in raw:
            if u == 1 and c == 0:
                cast("s", u, c0, piece, 0, width)
            elif u == 1 and c == 1:
                cast("v", u, c0, piece, 0, width)
            else:
                cast("v", u, c0, piece, 0, width * 5 // 8)
                cast("s", u, c0, piece, width * 5 // 8, width)
            if u == 0 and c == 1:
                for s in range(NS):
                    nc.vector.tensor_copy(out=lane[s % 3][:, 1 - s // 3, :], in_=pair[0][:].bitcast(U32).indirect(lists(s * SL, (s + 1) * SL)))

        woven = [keep.tile([P, 4 * SL], BF16, name=f"woven{s}", align_bytes=64) for s in range(NS)]
        codes = keep.tile([P, S], U32, name="codes", align_bytes=64)
        x_scale = keep.tile([P, S], U8, name="x_scale", align_bytes=64)
        bank = [psum.tile([P, 2, SL], F32, name=f"bank{s}", tag=f"bank0_{s}") for s in range(NS)]
        wide = [[psum.tile([P, 2 * SL], F32, name=f"wide{i}_{h}", tag=f"bank1_{2 * h + i}") for h in range(2)] for i in range(2)]
        gate = [keep.tile([P, S], F32, name=f"gate{m}") for m in range(2)]
        carry = [keep.tile([P, S], F32, name=f"carry{m}") for m in range(2)]
        made = [keep.tile([P, S], F32, name=f"made{m}") for m in range(2)]
        passed = [keep.tile([P, S], F32, name=f"passed{m}") for m in range(2)]
        result = [keep.tile([P, S], F32, name=f"result{m}") for m in range(2)]
        turned = keep.tile([P, S], F32, name="turned")

        def gather(s):
            nc.vector.tensor_copy(out=lane[s % 3][:, 2, :], in_=pair[1][:].bitcast(U32).indirect(lists(s * SL, (s + 1) * SL)))
            nc.scalar.copy(
                out=woven[s][:].bitcast(U32).rearrange("p (t u) -> p t u", u=2),
                in_=lane[s % 3][:, 1 - s // 3 : 3 : 1 + s // 3, :].rearrange("p u t -> p t u"),
            )

        def quantise(s):
            cols = slice(s * SL, (s + 1) * SL)
            nc.vector.quantize_mx(out=codes[:, cols].bitcast(FP8X4), scales=x_scale[:, cols], in_=woven[s][:])

        def sums(i, m, a, b):
            if m == 0:
                return bank[a // SL][:, i, :]
            return wide[i][a // (2 * SL)][:]

        def multiply(m, a, b):
            for i in (1, 0):
                nc.tensor.matmul_mx(
                    out=sums(i, m, a, b),
                    lhsT=w_code[i][:, m * P : (m + 1) * P].bitcast(FP8X4),
                    lhsT_scale=w_scale[:, i * N + m * P : i * N + (m + 1) * P],
                    rhs=codes[:, a:b].bitcast(FP8X4),
                    rhs_scale=x_scale[:, a:b],
                    start=True,
                    stop=True,
                )

        def gates(m, a, b):
            nc.scalar.activation(carry[m][:, a:b], sums(1, m, a, b), ACT.Sigmoid, scale=-1.0)
            nc.scalar.activation(gate[m][:, a:b], sums(1, m, a, b), ACT.Sigmoid)

        def highway(m, a, b):
            nc.vector.tensor_tensor(passed[m][:, a:b], res_sb[m][:].indirect(lists(a, b)), carry[m][:, a:b], ALU.mult)

        def layer(m, a, b):
            nc.vector.scalar_tensor_tensor(out=made[m][:, a:b], in0=sums(0, m, a, b), scalar=0.0, in1=gate[m][:, a:b], op0=ALU.max, op1=ALU.mult)

        def store(queue, m, a, b):
            queue.dma_start(out=out[m * P : (m + 1) * P, a:b], in_=result[m][:, a:b])

        def add_on_vector(m, a, b):
            nc.vector.tensor_tensor(result[m][:, a:b], passed[m][:, a:b], made[m][:, a:b], ALU.add)
            store(nc.sync, m, a, b)

        def sum_turned(m, h):
            summed = psum.tile([P, 2 * SL], F32, name=f"summed{m}_{h}", tag=f"bank{m}_{2 * h}")
            for j in range(4):
                cols = slice(2 * SL * h + P * j, 2 * SL * h + P * (j + 1))
                for first, term in ((True, passed[m]), (False, made[m])):
                    nc.tensor.matmul(summed[:, P * j : P * (j + 1)], lhsT=term[:, cols], rhs=ident[:], start=first, stop=not first, is_transpose=True)
            nc.scalar.copy(out=turned[:, 2 * SL * h : 2 * SL * (h + 1)], in_=summed[:])

        def turn_back(m, h):
            back = psum.tile([P, 2 * SL], F32, name=f"back{m}_{h}", tag=f"bank{m}_{2 * h + 1}")
            for j in range(4):
                cols = slice(2 * SL * h + P * j, 2 * SL * h + P * (j + 1))
                nc.tensor.transpose(back[:, P * j : P * (j + 1)], turned[:, cols], ident[:])
            nc.scalar.copy(out=result[m][:, 2 * SL * h : 2 * SL * (h + 1)], in_=back[:])
            store(nc.scalar, m, 2 * SL * h, 2 * SL * (h + 1))

        def terms(s):
            highway(0, s * SL, (s + 1) * SL)
            layer(0, s * SL, (s + 1) * SL)

        gather(0)
        gather(1)
        gather(2)
        quantise(0)
        multiply(0, 0, 256)
        gather(3)
        quantise(1)
        multiply(0, 256, 512)
        gates(0, 0, 256)
        quantise(2)
        multiply(0, 512, 768)
        terms(0)
        gates(0, 256, 512)
        quantise(3)
        multiply(0, 768, 1024)
        multiply(1, 0, 512)
        multiply(1, 512, 1024)
        terms(1)
        gates(0, 512, 768)
        terms(2)
        gates(0, 768, 1024)
        terms(3)
        gates(1, 0, 512)
        sum_turned(0, 0)
        highway(1, 0, 512)
        layer(1, 0, 512)
        gates(1, 512, 1024)
        turn_back(0, 0)
        sum_turned(0, 1)
        layer(1, 512, 1024)
        highway(1, 512, 896)
        add_on_vector(1, 0, 512)
        turn_back(0, 1)
        highway(1, 896, 1024)
        add_on_vector(1, 512, 896)
        add_on_vector(1, 896, 1024)
